import numpy as np
import ml_dtypes


def mxq(x, axis, fmt="e4m3"):
    dtype, down = {"e4m3": (ml_dtypes.float8_e4m3fn, 7), "e5m2": (ml_dtypes.float8_e5m2, 14)}[fmt]
    v = np.moveaxis(np.asarray(x, np.float32).astype(ml_dtypes.bfloat16).astype(np.float64), axis, -1)
    blocks = v.reshape(v.shape[:-1] + (-1, 32))
    amax = np.abs(blocks).max(-1, keepdims=True)
    byte = np.maximum(np.where(amax > 0, np.frexp(amax)[1] - 1 + 127, 0) - down, 1)
    scale = np.exp2(byte - 127.0)
    codes = (blocks / scale).astype(np.float32).astype(dtype).astype(np.float64)
    return np.moveaxis((codes * scale).reshape(v.shape), -1, axis)


WIDE = False


def mx_kscale(k):
    if not WIDE:
        return np.ones(k)
    levels = np.array([10, -10, 5, -5, 0])
    if k % 512:
        return np.exp2(np.random.permutation(np.resize(levels, k // 32))).repeat(32)
    a = np.empty((k // 512, 16))
    for p in range(k // 512):
        a[p, :8] = np.random.permutation(np.resize(levels, 8))
        for g in range(8):
            far = levels[np.abs(levels - a[p, g]) >= 10]
            a[p, g + 8] = far[np.random.randint(len(far))]
    return np.exp2(a.ravel()).repeat(32)


BF16 = ml_dtypes.bfloat16


def bf(x):
    return np.asarray(x, np.float32).astype(BF16)


def f64(x):
    return np.asarray(x).astype(np.float64)


E2M1 = np.array([0.0, 0.5, 1.0, 1.5, 2.0, 3.0, 4.0, 6.0, -0.0, -0.5, -1.0, -1.5, -2.0, -3.0, -4.0, -6.0])


def pack_weight(w, fmt):
    k, n = w.shape
    w = f64(bf(w)).reshape(k // 32, 32, n)
    amax = np.abs(w).max(1)
    if fmt == "e4m3":
        byte = np.frexp(amax)[1] - 1 + 127 - 7
    else:
        mant, ex = np.frexp(amax / 6.0)
        byte = np.where(mant > 0.5, ex, ex - 1) + 127
    byte = np.clip(np.where(amax > 0, byte, 1), 1, 254)
    scaled = (w * np.exp2(127.0 - byte)[:, None, :]).reshape(k, n).astype(np.float32)
    by_word = np.ascontiguousarray(scaled.reshape(k // 512, 128, 4, n).transpose(0, 1, 3, 2))
    if fmt == "e4m3":
        words = by_word.astype(ml_dtypes.float8_e4m3fn).view(np.uint8)
    else:
        c = by_word.astype(ml_dtypes.float4_e2m1fn).view(np.uint8) & 0xF
        words = c[..., 0::2] | (c[..., 1::2] << 4)
    return np.ascontiguousarray(words), np.ascontiguousarray(byte.astype(np.uint8).reshape(k // 512, 16, n))


def unpack_weight(words, scales, fmt):
    g, p, n, _ = words.shape
    if fmt == "e4m3":
        vals = np.ascontiguousarray(words).view(ml_dtypes.float8_e4m3fn).astype(np.float64)
    else:
        nib = np.empty((g, p, n, 4), np.uint8)
        nib[..., 0::2] = words & 0xF
        nib[..., 1::2] = words >> 4
        vals = E2M1[nib]
    vals = vals * np.repeat(np.exp2(scales.astype(np.float64) - 127.0), 8, axis=1)[..., None]
    return vals.transpose(0, 1, 3, 2).reshape(g * 512, n)

def planes(Y):
    n, m = Y.shape
    b = f64(bf(Y)).reshape(n // 32, 32, m)
    amax = np.abs(b).max(1)
    byte = np.clip(np.where(amax > 0, np.frexp(amax)[1] - 1 + 127 - 7, 1), 1, 254)
    codes = (b * np.exp2(127.0 - byte)[:, None, :]).reshape(n, m).astype(np.float32).astype(ml_dtypes.float8_e4m3fn).view(np.uint8)
    words = codes.reshape(n // 512, 128, 4, m).transpose(0, 1, 3, 2)
    return np.ascontiguousarray(words), np.ascontiguousarray(byte.astype(np.uint8).reshape(n // 512, 16, m))


B, P, Q, K, L = 8, 512, 512, 512, 512

TIKHONOV = 0.3


def tikhonov_filter(sl, sr):
    v = sl[:, None] * sr[None, :]
    return v / (v * v + TIKHONOV)


def setup_inputs():
    s, t = mx_kscale(P), mx_kscale(Q)
    y = bf(np.random.standard_normal((B, P, Q)) * s[None, :, None] * t[None, None, :])
    rg = bf(1.0 + 0.1 * np.random.standard_normal(P))
    ul_words, ul_scales = pack_weight(np.random.standard_normal((P, K)) / np.sqrt(P) / s[:, None], "e4m3")
    cg = bf(1.0 + 0.1 * np.random.standard_normal(Q))
    ur_words, ur_scales = pack_weight(np.random.standard_normal((Q, L)) / np.sqrt(Q) / t[:, None], "e4m3")
    return {
        "y": y,
        "rg": rg,
        "ul_words": ul_words,
        "ul_scales": ul_scales,
        "cg": cg,
        "ur_words": ur_words,
        "ur_scales": ur_scales,
        "sl": bf(np.random.uniform(0.5, 1.5, K)),
        "sr": bf(np.random.uniform(0.5, 1.5, L)),
    }


def core(y, rg, ul_words, ul_scales, cg, ur_words, ur_scales, sl, sr):
    a = f64(y) * f64(rg)[None, :, None]
    t = unpack_weight(ul_words, ul_scales, "e4m3").T @ mxq(a, 1, "e4m3")
    d = t * f64(cg)[None, None, :]
    m = mxq(d, 2, "e4m3") @ unpack_weight(ur_words, ur_scales, "e4m3")
    f = tikhonov_filter(f64(sl), f64(sr))
    return f[None, :, :] * m


def reference(y, rg, ul_words, ul_scales, cg, ur_words, ur_scales, sl, sr):
    R_out = core(y, rg, ul_words, ul_scales, cg, ur_words, ur_scales, sl, sr)
    words, scales = planes(np.moveaxis(R_out, 2, 0).reshape(512, -1))
    return R_out, words, scales

@@ -1,0 +1,335 @@
+from contextlib import ExitStack
+
+import concourse.mybir as mybir
+from concourse.masks import make_identity
+
+B, N = 8, 512
+P = 128
+PACK = 4
+TIKHONOV = 0.3
+FLOPS = 2 * 2 * B * N * N * N
+
+F32 = mybir.dt.float32
+BF16 = mybir.dt.bfloat16
+I32 = mybir.dt.int32
+U32 = mybir.dt.uint32
+U8 = mybir.dt.uint8
+FP8X4 = mybir.dt.float8_e4m3fn_x4
+ACT = mybir.ActivationFunctionType
+MUL = mybir.AluOpType.mult
+
+CHUNKS = 4 * B
+ON_SCALAR = tuple(s for s in range(CHUNKS) if s % 2 == 1 and s > 4 and s % 16 != 7)
+
+
+def tile_separablelenslesstikhonovcoefficients_x2_kernel(
+    tc, y, rg, ul_words, ul_scales, cg, ur_words, ur_scales, sl, sr, out_0, out_1, out_2
+):
+    nc = tc.nc
+    with ExitStack() as ctx:
+        const = ctx.enter_context(tc.tile_pool(name="const", bufs=1))
+        ypool = ctx.enter_context(tc.tile_pool(name="ypool", bufs=8))
+        work = ctx.enter_context(tc.tile_pool(name="work", bufs=2))
+        deep = ctx.enter_context(tc.tile_pool(name="deep", bufs=4))
+        psum = ctx.enter_context(tc.psum_pool(name="psum", bufs=2))
+        ctx.enter_context(tc.manual_schedule())
+
+        ident = const.tile([P, P], F32, name="ident")
+        rows = const.tile([P, P], BF16, name="rows")
+        rows_f = const.tile([P, P], F32, name="rows_f")
+        cols = const.tile([P, 16], F32, name="cols")
+        rg4 = const.tile([P, PACK], BF16, name="rg4")
+        cg4 = const.tile([P, PACK], BF16, name="cg4")
+        ul_c = const.tile([P, N], U32, name="ul_c", align_bytes=64)
+        ul_s = const.tile([P, N], U8, name="ul_s", align_bytes=64)
+        ur_c = const.tile([P, N], U32, name="ur_c", align_bytes=64)
+        ur_s = const.tile([P, N], U8, name="ur_s", align_bytes=64)
+        filt = const.tile([P, 4, N], F32, name="filt")
+        p_scales = const.tile([P, B * N], U8, name="p_scales", align_bytes=64)
+
+        nc.vector.memset(rows[:], 0.0)
+        nc.vector.memset(ul_s[:].bitcast(I32), 0)
+        nc.vector.memset(ur_s[:].bitcast(I32), 0)
+        make_identity(nc, ident[:])
+
+        def load_scales(queue, tile, dram):
+            for q in range(4):
+                queue.dma_start(
+                    out=tile[32 * q : 32 * q + 4, :].bitcast(I32),
+                    in_=dram[0, 4 * q : 4 * q + 4, :].bitcast(I32),
+                )
+
+        def load_words(queue, tile, dram):
+            queue.dma_start(out=tile[:].bitcast(I32), in_=dram[0].rearrange("p n t -> p (n t)").bitcast(I32))
+
+        y_t = {}
+
+        def load_y(b, pieces=1):
+            yt = ypool.tile([P, PACK, N], BF16, name="yt")
+            y_t[b] = yt
+            view = y[b].rearrange("(p j) q -> p j q", j=PACK)
+            step = PACK // pieces
+            for i in range(pieces):
+                nc.sync.dma_start(out=yt[:, i * step : (i + 1) * step, :], in_=view[:, i * step : (i + 1) * step, :])
+
+        nc.scalar.dma_start(out=rg4[:], in_=rg.rearrange("(p j) -> p j", j=PACK))
+        nc.scalar.dma_start(out=rows[0:4, :], in_=sl.rearrange("(t m) -> t m", m=P))
+        nc.scalar.dma_start(out=rows[4:8, :], in_=sr.rearrange("(t m) -> t m", m=P))
+        load_y(0, 4)
+        load_words(nc.sync, ul_c, ul_words)
+        nc.gpsimd.dma_start(out=cg4[:], in_=cg.rearrange("(p j) -> p j", j=PACK))
+        load_scales(nc.sync, ul_s, ul_scales)
+        load_y(1)
+        load_scales(nc.sync, ur_s, ur_scales)
+        load_words(nc.sync, ur_c, ur_words)
+        for b in range(2, B):
+            load_y(b)
+
+        a_s, a_g, a_c, a_sc = {}, {}, {}, {}
+
+        def scale_rows(b, j):
+            if j == 0:
+                a_s[b] = work.tile([P, PACK, N], BF16, name="a_scaled")
+            nc.vector.tensor_scalar(
+                out=a_s[b][:, j, :], in0=y_t[b][:, j, :], scalar1=rg4[:, j : j + 1], scalar2=None, op0=MUL
+            )
+
+        def interleave(b, h, copy):
+            if h == 0:
+                a_g[b] = work.tile([P, PACK * N], BF16, name="a_grouped", align_bytes=64)
+            m = slice(32 * h, 32 * h + 32)
+            copy(
+                out=a_g[b][:].rearrange("p (t m j) -> p m j t", t=4, j=PACK)[:, m, :, :],
+                in_=a_s[b][:].rearrange("p j (m t) -> p m j t", t=4)[:, m, :, :],
+            )
+
+        def quant_a(b):
+            a_c[b] = work.tile([P, N], U32, name="a_codes", align_bytes=64)
+            a_sc[b] = work.tile([P, N], U8, name="a_scales", align_bytes=64)
+            nc.vector.quantize_mx(out=a_c[b][:].bitcast(FP8X4), scales=a_sc[b][:], in_=a_g[b][:])
+
+        t_ps, d_g, d_c, d_sc, m_ps, r_f, r_b, x_ps, p_g = {}, {}, {}, {}, {}, {}, {}, {}, {}
+
+        def mx1(s):
+            b, T = divmod(s, 4)
+            t_ps[s] = psum.tile([P, 4, P], F32, name="t_ps", bufs=4)
+            k = slice(T * P, T * P + P)
+            for t in range(4):
+                q = slice(t * P, t * P + P)
+                nc.tensor.matmul_mx(
+                    out=t_ps[s][:, t, :],
+                    lhsT=a_c[b][:, q].bitcast(FP8X4),
+                    lhsT_scale=a_sc[b][:, q],
+                    rhs=ul_c[:, k].bitcast(FP8X4),
+                    rhs_scale=ul_s[:, k],
+                    start=True,
+                    stop=True,
+                )
+
+        def make_d(s):
+            pair, c = divmod(s, 2)
+            if c == 0:
+                d_g[pair] = work.tile([P, 2, P, PACK], BF16, name="d_grouped", align_bytes=64, bufs=3)
+            if s in ON_SCALAR:
+                d_t = work.tile([P, PACK, P], BF16, name="d_t")
+                for t in range(4):
+                    nc.scalar.activation(
+                        out=d_t[:, t, :], in_=t_ps[s][:, t, :], func=ACT.Copy, scale=cg4f[:, t : t + 1]
+                    )
+                nc.scalar.copy(out=d_g[pair][:, c, :, :], in_=d_t[:].rearrange("p t k -> p k t"))
+            else:
+                nc.vector.tensor_tensor(
+                    out=d_g[pair][:, c, :, :],
+                    in0=t_ps[s][:].rearrange("p t k -> p k t"),
+                    in1=cg4[:].unsqueeze(1).to_broadcast([P, P, PACK]),
+                    op=MUL,
+                )
+
+        def quant_d(pair):
+            d_c[pair] = work.tile([P, 2 * P], U32, name="d_codes", align_bytes=64, bufs=3)
+            d_sc[pair] = work.tile([P, 2 * P], U8, name="d_scales", align_bytes=64, bufs=3)
+            nc.vector.quantize_mx(
+                out=d_c[pair][:].bitcast(FP8X4),
+                scales=d_sc[pair][:],
+                in_=d_g[pair][:].rearrange("p c k t -> p (c k t)"),
+            )
+
+        def mx2(s):
+            pair, c = divmod(s, 2)
+            k = slice(c * P, c * P + P)
+            m_ps[s] = psum.tile([P, N], F32, name="m_ps", bufs=2)
+            nc.tensor.matmul_mx(
+                out=m_ps[s][:],
+                lhsT=d_c[pair][:, k].bitcast(FP8X4),
+                lhsT_scale=d_sc[pair][:, k],
+                rhs=ur_c[:].bitcast(FP8X4),
+                rhs_scale=ur_s[:],
+                start=True,
+                stop=True,
+            )
+
+        def filter_out(s):
+            pair, c = divmod(s, 2)
+            if c == 0:
+                r_f[pair] = deep.tile([P, 2, N], F32, name="r_f")
+            nc.vector.scalar_tensor_tensor(
+                out=r_f[pair][:, c, :],
+                in0=m_ps[s][:],
+                scalar=cols[:, s % 4 : s % 4 + 1],
+                in1=filt[:, s % 4, :],
+                op0=MUL,
+                op1=MUL,
+            )
+
+        def round_out(s):
+            pair, c = divmod(s, 2)
+            if c == 0:
+                r_b[pair] = deep.tile([P, 2, N], BF16, name="r_b")
+            nc.gpsimd.tensor_scalar(
+                out=r_b[pair][:, c, :], in0=r_f[pair][:, c, :], scalar1=1.0, scalar2=1.0, op0=MUL, op1=MUL
+            )
+
+        def store_out(pair):
+            b, h = divmod(pair, 2)
+            nc.sync.dma_start(
+                out=out_0[b, 2 * P * h : 2 * P * h + 2 * P, :].rearrange("(c k) l -> k c l", c=2),
+                in_=r_f[pair][:],
+            )
+
+        def turn(pair):
+            x_ps[pair] = psum.tile([P, 2, 2, P], F32, name="x_ps", bufs=2)
+            for c in range(2):
+                words = r_b[pair][:, c, :].bitcast(F32)
+                for u in range(2):
+                    nc.tensor.transpose(x_ps[pair][:, c, u, :], words[:, u::2], ident[:])
+
+        def gather_out(pair):
+            p_g[pair] = deep.tile([P, 2 * P * PACK], BF16, name="p_grouped", align_bytes=64)
+            nc.scalar.copy(
+                out=p_g[pair][:].bitcast(F32).rearrange("p (c k u) -> p c k u", c=2, u=2),
+                in_=x_ps[pair][:].rearrange("p c u k -> p c k u"),
+            )
+
+        p_c = {}
+
+        def quant_out(pair):
+            b, h = divmod(pair, 2)
+            if h == 0:
+                p_c[b] = work.tile([P, N], U32, name="p_codes", align_bytes=64)
+            m0 = b * N + h * 2 * P
+            nc.vector.quantize_mx(
+                out=p_c[b][:, 2 * P * h : 2 * P * h + 2 * P].bitcast(FP8X4),
+                scales=p_scales[:, m0 : m0 + 2 * P],
+                in_=p_g[pair][:],
+            )
+
+        def store_codes(b):
+            nc.sync.dma_start(
+                out=out_1[0].rearrange("p m t -> p (m t)")[:, 4 * N * b : 4 * N * (b + 1)].bitcast(I32),
+                in_=p_c[b][:].bitcast(I32),
+            )
+
+        def store_scales(b0, b1):
+            for q in range(4):
+                nc.sync.dma_start(
+                    out=out_2[0, 4 * q : 4 * q + 4, N * b0 : N * b1].bitcast(I32),
+                    in_=p_scales[32 * q : 32 * q + 4, N * b0 : N * b1].bitcast(I32),
+                )
+
+        vcopy, scopy = nc.vector.tensor_copy, nc.scalar.copy
+        for j in range(4):
+            scale_rows(0, j)
+        cg4f = const.tile([P, PACK], F32, name="cg4f")
+        nc.vector.tensor_copy(out=rows_f[:], in_=rows[:])
+        c_ps = psum.tile([P, P], F32, name="c_ps", tag="m_ps", bufs=2)
+        nc.tensor.transpose(c_ps[:], rows_f[:], ident[:])
+        nc.vector.tensor_copy(out=cols[:, 0:8], in_=c_ps[:, 0:8])
+        nc.vector.tensor_tensor(out=cols[:, 8:16], in0=cols[:, 0:8], in1=cols[:, 0:8], op=MUL)
+        nc.vector.tensor_copy(out=cg4f[:], in_=cg4[:])
+        sr2_ps = psum.tile([P, N], F32, name="sr2_ps", tag="x_ps", bufs=2)
+        sr_ps = psum.tile([P, N], F32, name="sr_ps", tag="x_ps", bufs=2)
+        for t in range(4):
+            nc.tensor.transpose(
+                sr2_ps[:, P * t : P * t + P], cols[:, 12 + t : 13 + t].to_broadcast([P, P]), ident[:]
+            )
+        for t in range(4):
+            nc.tensor.transpose(sr_ps[:, P * t : P * t + P], cols[:, 4 + t : 5 + t].to_broadcast([P, P]), ident[:])
+        inv = const.tile([P, 4, N], F32, name="inv")
+
+        def invert(t):
+            nc.scalar.activation(
+                out=inv[:, t, :],
+                in_=sr2_ps[:],
+                func=ACT.Abs_reciprocal_sqrt,
+                bias=TIKHONOV,
+                scale=cols[:, 8 + t : 9 + t],
+            )
+
+        def square(t):
+            nc.scalar.activation(out=inv[:, t, :], in_=inv[:, t, :], func=ACT.Square)
+
+        def make_filter(t):
+            nc.vector.tensor_tensor(out=filt[:, t, :], in0=sr_ps[:], in1=inv[:, t, :], op=MUL)
+
+        for h in range(4):
+            interleave(0, h, vcopy)
+        invert(0)
+        square(0)
+        make_filter(0)
+        quant_a(0)
+        for j in range(4):
+            scale_rows(1, j)
+        for h in range(2):
+            interleave(1, h, vcopy)
+        interleave(1, 2, scopy)
+        invert(1)
+        square(1)
+        interleave(1, 3, scopy)
+        invert(2)
+        square(2)
+        invert(3)
+        square(3)
+
+        PAIRS = CHUNKS // 2
+        for i in range(-3, PAIRS + 2):
+            if 0 <= i - 1 < PAIRS:
+                turn(i - 1)
+            for c in range(2):
+                if 0 <= i < PAIRS:
+                    filter_out(2 * i + c)
+                    round_out(2 * i + c)
+            if 0 <= i < PAIRS:
+                store_out(i)
+            if 0 <= i + 2 < PAIRS:
+                make_d(2 * i + 4)
+                make_d(2 * i + 5)
+            if 0 <= i + 1 < PAIRS:
+                quant_d(i + 1)
+                mx2(2 * i + 2)
+                mx2(2 * i + 3)
+            if i in (-1, 0):
+                for t in (1,) if i < 0 else (2, 3):
+                    make_filter(t)
+            if 0 <= i - 2 < PAIRS:
+                quant_out(i - 2)
+                b, h = divmod(i - 2, 2)
+                if h == 1:
+                    store_codes(b)
+                    if b in (3, 5, 6, 7):
+                        store_scales({3: 0, 5: 4, 6: 6, 7: 7}[b], b + 1)
+            if i % 2 == 1 and 1 <= (i + 3) // 2 < B:
+                quant_a((i + 3) // 2)
+            if 0 <= i + 3 < PAIRS:
+                mx1(2 * i + 6)
+                mx1(2 * i + 7)
+            if 0 <= i - 1 < PAIRS:
+                gather_out(i - 1)
+            nb, h = divmod(i + 5, 2)
+            if 1 <= nb < B:
+                for hh in (2 * h, 2 * h + 1):
+                    if nb > 1:
+                        interleave(nb, hh, scopy)
+            nb, h = divmod(i + 7, 2)
+            if 2 <= nb < B:
+                scale_rows(nb, 2 * h)
+                scale_rows(nb, 2 * h + 1)

@@ -3,9 +3,11 @@ from contextlib import ExitStack
 import concourse.mybir as mybir
 from concourse.masks import make_identity
 
-B, N = 8, 512
+B = 8
+N = 512
 P = 128
-PACK = 4
+WORD = 4
+BLOCKS = N // P
 TIKHONOV = 0.3
 FLOPS = 2 * 2 * B * N * N * N
 
@@ -16,10 +18,17 @@ U32 = mybir.dt.uint32
 U8 = mybir.dt.uint8
 FP8X4 = mybir.dt.float8_e4m3fn_x4
 ACT = mybir.ActivationFunctionType
-MUL = mybir.AluOpType.mult
+MULT = mybir.AluOpType.mult
 
-CHUNKS = 4 * B
-ON_SCALAR = tuple(s for s in range(CHUNKS) if s % 2 == 1 and s > 4 and s % 16 != 7)
+BLOCK_ORDER = (3, 0, 1, 2)
+
+
+def scalar_blocks(b):
+    if b == 0:
+        return ()
+    if b >= B - 2:
+        return (3, 2)
+    return (3,)
 
 
 def tile_separablelenslesstikhonovcoefficients_x2_kernel(
@@ -28,308 +37,358 @@ def tile_separablelenslesstikhonovcoefficients_x2_kernel(
     nc = tc.nc
     with ExitStack() as ctx:
         const = ctx.enter_context(tc.tile_pool(name="const", bufs=1))
-        ypool = ctx.enter_context(tc.tile_pool(name="ypool", bufs=8))
+        loads = ctx.enter_context(tc.tile_pool(name="loads", bufs=B))
         work = ctx.enter_context(tc.tile_pool(name="work", bufs=2))
-        deep = ctx.enter_context(tc.tile_pool(name="deep", bufs=4))
         psum = ctx.enter_context(tc.psum_pool(name="psum", bufs=2))
         ctx.enter_context(tc.manual_schedule())
 
-        ident = const.tile([P, P], F32, name="ident")
-        rows = const.tile([P, P], BF16, name="rows")
-        rows_f = const.tile([P, P], F32, name="rows_f")
-        cols = const.tile([P, 16], F32, name="cols")
-        rg4 = const.tile([P, PACK], BF16, name="rg4")
-        cg4 = const.tile([P, PACK], BF16, name="cg4")
-        ul_c = const.tile([P, N], U32, name="ul_c", align_bytes=64)
-        ul_s = const.tile([P, N], U8, name="ul_s", align_bytes=64)
-        ur_c = const.tile([P, N], U32, name="ur_c", align_bytes=64)
-        ur_s = const.tile([P, N], U8, name="ur_s", align_bytes=64)
-        filt = const.tile([P, 4, N], F32, name="filt")
-        p_scales = const.tile([P, B * N], U8, name="p_scales", align_bytes=64)
+        identity = const.tile([P, P], F32, name="identity")
+        vectors = const.tile([P, P], BF16, name="vectors")
+        vectors_f32 = const.tile([P, P], F32, name="vectors_f32")
+        columns = const.tile([P, 16], F32, name="columns")
+        rg_words = const.tile([P, WORD], BF16, name="rg_words")
+        cg_words = const.tile([P, WORD], BF16, name="cg_words")
+        cg_f32 = const.tile([P, WORD], F32, name="cg_f32")
+        ul_codes = const.tile([P, N], U32, name="ul_codes", align_bytes=64)
+        ul_plane = const.tile([P, N], U8, name="ul_plane", align_bytes=64)
+        ur_codes = const.tile([P, N], U32, name="ur_codes", align_bytes=64)
+        ur_plane = const.tile([P, N], U8, name="ur_plane", align_bytes=64)
+        inverse = const.tile([P, BLOCKS, N], F32, name="inverse")
+        gain = const.tile([P, BLOCKS, N], F32, name="gain")
+        out_plane = const.tile([P, B * N], U8, name="out_plane", align_bytes=64)
 
-        nc.vector.memset(rows[:], 0.0)
-        nc.vector.memset(ul_s[:].bitcast(I32), 0)
-        nc.vector.memset(ur_s[:].bitcast(I32), 0)
-        make_identity(nc, ident[:])
+        nc.vector.memset(vectors[:], 0.0)
+        nc.vector.memset(ul_plane[:].bitcast(I32), 0)
+        nc.vector.memset(ur_plane[:].bitcast(I32), 0)
+        make_identity(nc, identity[:])
 
-        def load_scales(queue, tile, dram):
-            for q in range(4):
+        y_rows = {}
+
+        def load_image(b, pieces):
+            y_tile = loads.tile([P, WORD, N], BF16, name="y_tile")
+            y_rows[b] = y_tile
+            rows = y[b].rearrange("(i j) q -> i j q", j=WORD)
+            step = WORD // pieces
+            for j in range(0, WORD, step):
+                nc.sync.dma_start(out=y_tile[:, j : j + step, :], in_=rows[:, j : j + step, :])
+
+        def load_words(codes, dram):
+            nc.sync.dma_start(out=codes[:].bitcast(I32), in_=dram[0].rearrange("i n t -> i (n t)").bitcast(I32))
+
+        def load_scales(queue, plane, dram):
+            for quadrant in range(4):
                 queue.dma_start(
-                    out=tile[32 * q : 32 * q + 4, :].bitcast(I32),
-                    in_=dram[0, 4 * q : 4 * q + 4, :].bitcast(I32),
+                    out=plane[32 * quadrant : 32 * quadrant + 4, :].bitcast(I32),
+                    in_=dram[0, 4 * quadrant : 4 * quadrant + 4, :].bitcast(I32),
                 )
 
-        def load_words(queue, tile, dram):
-            queue.dma_start(out=tile[:].bitcast(I32), in_=dram[0].rearrange("p n t -> p (n t)").bitcast(I32))
-
-        y_t = {}
-
-        def load_y(b, pieces=1):
-            yt = ypool.tile([P, PACK, N], BF16, name="yt")
-            y_t[b] = yt
-            view = y[b].rearrange("(p j) q -> p j q", j=PACK)
-            step = PACK // pieces
-            for i in range(pieces):
-                nc.sync.dma_start(out=yt[:, i * step : (i + 1) * step, :], in_=view[:, i * step : (i + 1) * step, :])
-
-        nc.scalar.dma_start(out=rg4[:], in_=rg.rearrange("(p j) -> p j", j=PACK))
-        nc.scalar.dma_start(out=rows[0:4, :], in_=sl.rearrange("(t m) -> t m", m=P))
-        nc.scalar.dma_start(out=rows[4:8, :], in_=sr.rearrange("(t m) -> t m", m=P))
-        load_y(0, 4)
-        load_words(nc.sync, ul_c, ul_words)
-        nc.gpsimd.dma_start(out=cg4[:], in_=cg.rearrange("(p j) -> p j", j=PACK))
-        load_scales(nc.sync, ul_s, ul_scales)
-        load_y(1)
-        load_scales(nc.sync, ur_s, ur_scales)
-        load_words(nc.sync, ur_c, ur_words)
+        nc.scalar.dma_start(out=rg_words[:], in_=rg.rearrange("(i j) -> i j", j=WORD))
+        nc.scalar.dma_start(out=vectors[0:4, :], in_=sl.rearrange("(r c) -> r c", c=P))
+        nc.scalar.dma_start(out=vectors[4:8, :], in_=sr.rearrange("(r c) -> r c", c=P))
+        load_image(0, WORD)
+        load_words(ul_codes, ul_words)
+        nc.gpsimd.dma_start(out=cg_words[:], in_=cg.rearrange("(i j) -> i j", j=WORD))
+        load_scales(nc.sync, ul_plane, ul_scales)
+        load_image(1, 1)
+        load_words(ur_codes, ur_words)
+        load_scales(nc.gpsimd, ur_plane, ur_scales)
         for b in range(2, B):
-            load_y(b)
+            load_image(b, 1)
 
-        a_s, a_g, a_c, a_sc = {}, {}, {}, {}
+        a_scaled, a_grouped, a_codes, a_plane = {}, {}, {}, {}
 
-        def scale_rows(b, j):
-            if j == 0:
-                a_s[b] = work.tile([P, PACK, N], BF16, name="a_scaled")
-            nc.vector.tensor_scalar(
-                out=a_s[b][:, j, :], in0=y_t[b][:, j, :], scalar1=rg4[:, j : j + 1], scalar2=None, op0=MUL
-            )
+        def scale_rows(b):
+            a_scaled[b] = work.tile([P, WORD, N], BF16, name="a_scaled", bufs=3)
+            for j in range(WORD):
+                nc.vector.tensor_scalar(
+                    out=a_scaled[b][:, j, :],
+                    in0=y_rows[b][:, j, :],
+                    scalar1=rg_words[:, j : j + 1],
+                    scalar2=None,
+                    op0=MULT,
+                )
 
-        def interleave(b, h, copy):
-            if h == 0:
-                a_g[b] = work.tile([P, PACK * N], BF16, name="a_grouped", align_bytes=64)
-            m = slice(32 * h, 32 * h + 32)
+        def group_rows(b, half, copy):
+            if half == 0:
+                a_grouped[b] = work.tile([P, WORD * N], BF16, name="a_grouped", align_bytes=64, bufs=3)
+            i = slice(64 * half, 64 * half + 64)
             copy(
-                out=a_g[b][:].rearrange("p (t m j) -> p m j t", t=4, j=PACK)[:, m, :, :],
-                in_=a_s[b][:].rearrange("p j (m t) -> p m j t", t=4)[:, m, :, :],
+                out=a_grouped[b][:].rearrange("p (t i j) -> p i j t", t=WORD, j=WORD)[:, i, :, :],
+                in_=a_scaled[b][:].rearrange("p j (i t) -> p i j t", t=WORD)[:, i, :, :],
             )
 
-        def quant_a(b):
-            a_c[b] = work.tile([P, N], U32, name="a_codes", align_bytes=64)
-            a_sc[b] = work.tile([P, N], U8, name="a_scales", align_bytes=64)
-            nc.vector.quantize_mx(out=a_c[b][:].bitcast(FP8X4), scales=a_sc[b][:], in_=a_g[b][:])
+        def quantize_a(b):
+            a_codes[b] = work.tile([P, N], U32, name="a_codes", align_bytes=64)
+            a_plane[b] = work.tile([P, N], U8, name="a_plane", align_bytes=64)
+            nc.vector.quantize_mx(out=a_codes[b][:].bitcast(FP8X4), scales=a_plane[b][:], in_=a_grouped[b][:])
 
-        t_ps, d_g, d_c, d_sc, m_ps, r_f, r_b, x_ps, p_g = {}, {}, {}, {}, {}, {}, {}, {}, {}
+        t_psum, d_grouped, d_codes, d_plane = {}, {}, {}, {}
 
-        def mx1(s):
-            b, T = divmod(s, 4)
-            t_ps[s] = psum.tile([P, 4, P], F32, name="t_ps", bufs=4)
-            k = slice(T * P, T * P + P)
-            for t in range(4):
-                q = slice(t * P, t * P + P)
+        def first_matmul(b, block):
+            t_psum[b, block] = psum.tile([P, WORD, P], F32, name="t_psum", bufs=3)
+            k = slice(P * block, P * block + P)
+            for t in range(WORD):
+                columns_q = slice(P * t, P * t + P)
                 nc.tensor.matmul_mx(
-                    out=t_ps[s][:, t, :],
-                    lhsT=a_c[b][:, q].bitcast(FP8X4),
-                    lhsT_scale=a_sc[b][:, q],
-                    rhs=ul_c[:, k].bitcast(FP8X4),
-                    rhs_scale=ul_s[:, k],
+                    out=t_psum[b, block][:, t, :],
+                    lhsT=a_codes[b][:, columns_q].bitcast(FP8X4),
+                    lhsT_scale=a_plane[b][:, columns_q],
+                    rhs=ul_codes[:, k].bitcast(FP8X4),
+                    rhs_scale=ul_plane[:, k],
                     start=True,
                     stop=True,
                 )
 
-        def make_d(s):
-            pair, c = divmod(s, 2)
-            if c == 0:
-                d_g[pair] = work.tile([P, 2, P, PACK], BF16, name="d_grouped", align_bytes=64, bufs=3)
-            if s in ON_SCALAR:
-                d_t = work.tile([P, PACK, P], BF16, name="d_t")
-                for t in range(4):
-                    nc.scalar.activation(
-                        out=d_t[:, t, :], in_=t_ps[s][:, t, :], func=ACT.Copy, scale=cg4f[:, t : t + 1]
-                    )
-                nc.scalar.copy(out=d_g[pair][:, c, :, :], in_=d_t[:].rearrange("p t k -> p k t"))
-            else:
-                nc.vector.tensor_tensor(
-                    out=d_g[pair][:, c, :, :],
-                    in0=t_ps[s][:].rearrange("p t k -> p k t"),
-                    in1=cg4[:].unsqueeze(1).to_broadcast([P, P, PACK]),
-                    op=MUL,
-                )
+        def d_block(b, block):
+            if b not in d_grouped:
+                d_grouped[b] = work.tile([P, N, WORD], BF16, name="d_grouped", align_bytes=64)
+            return d_grouped[b][:, P * block : P * block + P, :]
 
-        def quant_d(pair):
-            d_c[pair] = work.tile([P, 2 * P], U32, name="d_codes", align_bytes=64, bufs=3)
-            d_sc[pair] = work.tile([P, 2 * P], U8, name="d_scales", align_bytes=64, bufs=3)
-            nc.vector.quantize_mx(
-                out=d_c[pair][:].bitcast(FP8X4),
-                scales=d_sc[pair][:],
-                in_=d_g[pair][:].rearrange("p c k t -> p (c k t)"),
+        def make_d_vector(b, block):
+            nc.vector.tensor_tensor(
+                out=d_block(b, block),
+                in0=t_psum[b, block][:].rearrange("p t k -> p k t"),
+                in1=cg_words[:].unsqueeze(1).to_broadcast([P, P, WORD]),
+                op=MULT,
             )
 
-        def mx2(s):
-            pair, c = divmod(s, 2)
-            k = slice(c * P, c * P + P)
-            m_ps[s] = psum.tile([P, N], F32, name="m_ps", bufs=2)
+        def make_d_scalar(b, block):
+            d_rows = work.tile([P, WORD, P], BF16, name="d_rows")
+            for t in range(WORD):
+                nc.scalar.activation(
+                    out=d_rows[:, t, :], in_=t_psum[b, block][:, t, :], func=ACT.Copy, scale=cg_f32[:, t : t + 1]
+                )
+            nc.scalar.copy(out=d_block(b, block), in_=d_rows[:].rearrange("p t k -> p k t"))
+
+        def make_d(b, block):
+            if block in scalar_blocks(b):
+                make_d_scalar(b, block)
+            else:
+                make_d_vector(b, block)
+
+        def quantize_d(b):
+            d_codes[b] = work.tile([P, N], U32, name="d_codes", align_bytes=64)
+            d_plane[b] = work.tile([P, N], U8, name="d_plane", align_bytes=64)
+            nc.vector.quantize_mx(
+                out=d_codes[b][:].bitcast(FP8X4),
+                scales=d_plane[b][:],
+                in_=d_grouped[b][:].rearrange("p k t -> p (k t)"),
+            )
+
+        m_psum, result, rounded = {}, {}, {}
+
+        def second_matmul(b, block):
+            k = slice(P * block, P * block + P)
+            m_psum[b, block] = psum.tile([P, N], F32, name="m_psum", bufs=3)
             nc.tensor.matmul_mx(
-                out=m_ps[s][:],
-                lhsT=d_c[pair][:, k].bitcast(FP8X4),
-                lhsT_scale=d_sc[pair][:, k],
-                rhs=ur_c[:].bitcast(FP8X4),
-                rhs_scale=ur_s[:],
+                out=m_psum[b, block][:],
+                lhsT=d_codes[b][:, k].bitcast(FP8X4),
+                lhsT_scale=d_plane[b][:, k],
+                rhs=ur_codes[:].bitcast(FP8X4),
+                rhs_scale=ur_plane[:],
                 start=True,
                 stop=True,
             )
 
-        def filter_out(s):
-            pair, c = divmod(s, 2)
-            if c == 0:
-                r_f[pair] = deep.tile([P, 2, N], F32, name="r_f")
+        def filter_block(b, block):
+            if block == 0:
+                result[b] = work.tile([P, BLOCKS, N], F32, name="result", bufs=3)
+                rounded[b] = work.tile([P, BLOCKS, N], BF16, name="rounded")
             nc.vector.scalar_tensor_tensor(
-                out=r_f[pair][:, c, :],
-                in0=m_ps[s][:],
-                scalar=cols[:, s % 4 : s % 4 + 1],
-                in1=filt[:, s % 4, :],
-                op0=MUL,
-                op1=MUL,
+                out=result[b][:, block, :],
+                in0=m_psum[b, block][:],
+                scalar=columns[:, block : block + 1],
+                in1=gain[:, block, :],
+                op0=MULT,
+                op1=MULT,
             )
 
-        def round_out(s):
-            pair, c = divmod(s, 2)
-            if c == 0:
-                r_b[pair] = deep.tile([P, 2, N], BF16, name="r_b")
+        def store_result(b, block, count):
+            nc.sync.dma_start(
+                out=out_0[b, P * block : P * (block + count), :].rearrange("(c k) l -> k c l", c=count),
+                in_=result[b][:, block : block + count, :],
+            )
+
+        turned, p_grouped, p_codes = {}, {}, {}
+
+        def round_scalar(b, block):
+            nc.scalar.copy(out=rounded[b][:, block, :], in_=result[b][:, block, :])
+
+        def round_gpsimd(b, block):
             nc.gpsimd.tensor_scalar(
-                out=r_b[pair][:, c, :], in0=r_f[pair][:, c, :], scalar1=1.0, scalar2=1.0, op0=MUL, op1=MUL
+                out=rounded[b][:, block, :],
+                in0=result[b][:, block, :],
+                scalar1=1.0,
+                scalar2=1.0,
+                op0=MULT,
+                op1=MULT,
             )
 
-        def store_out(pair):
-            b, h = divmod(pair, 2)
-            nc.sync.dma_start(
-                out=out_0[b, 2 * P * h : 2 * P * h + 2 * P, :].rearrange("(c k) l -> k c l", c=2),
-                in_=r_f[pair][:],
-            )
-
-        def turn(pair):
-            x_ps[pair] = psum.tile([P, 2, 2, P], F32, name="x_ps", bufs=2)
-            for c in range(2):
-                words = r_b[pair][:, c, :].bitcast(F32)
+        def turn(b, block, count):
+            turned[b, block] = psum.tile([P, count, 2, P], F32, name="turned", bufs=2)
+            for c in range(count):
+                words = rounded[b][:, block + c, :].bitcast(F32)
                 for u in range(2):
-                    nc.tensor.transpose(x_ps[pair][:, c, u, :], words[:, u::2], ident[:])
+                    nc.tensor.transpose(turned[b, block][:, c, u, :], words[:, u::2], identity[:])
 
-        def gather_out(pair):
-            p_g[pair] = deep.tile([P, 2 * P * PACK], BF16, name="p_grouped", align_bytes=64)
+        def group_out(b, block, count):
+            if block == 0:
+                p_grouped[b] = work.tile([P, N * WORD], BF16, name="p_grouped", align_bytes=64)
+            values = slice(P * WORD * block, P * WORD * (block + count))
             nc.scalar.copy(
-                out=p_g[pair][:].bitcast(F32).rearrange("p (c k u) -> p c k u", c=2, u=2),
-                in_=x_ps[pair][:].rearrange("p c u k -> p c k u"),
+                out=p_grouped[b][:, values].bitcast(F32).rearrange("p (c k u) -> p c k u", c=count, u=2),
+                in_=turned[b, block][:].rearrange("p c u k -> p c k u"),
             )
 
-        p_c = {}
-
-        def quant_out(pair):
-            b, h = divmod(pair, 2)
-            if h == 0:
-                p_c[b] = work.tile([P, N], U32, name="p_codes", align_bytes=64)
-            m0 = b * N + h * 2 * P
+        def quantize_out(b, block, count):
+            if block == 0:
+                p_codes[b] = work.tile([P, N], U32, name="p_codes", align_bytes=64)
+            k = slice(P * block, P * (block + count))
             nc.vector.quantize_mx(
-                out=p_c[b][:, 2 * P * h : 2 * P * h + 2 * P].bitcast(FP8X4),
-                scales=p_scales[:, m0 : m0 + 2 * P],
-                in_=p_g[pair][:],
+                out=p_codes[b][:, k].bitcast(FP8X4),
+                scales=out_plane[:, b * N + P * block : b * N + P * (block + count)],
+                in_=p_grouped[b][:, P * WORD * block : P * WORD * (block + count)],
             )
 
-        def store_codes(b):
+        def store_codes(b, block, count):
+            first, last = b * N + P * block, b * N + P * (block + count)
             nc.sync.dma_start(
-                out=out_1[0].rearrange("p m t -> p (m t)")[:, 4 * N * b : 4 * N * (b + 1)].bitcast(I32),
-                in_=p_c[b][:].bitcast(I32),
+                out=out_1[0].rearrange("i m t -> i (m t)")[:, WORD * first : WORD * last].bitcast(I32),
+                in_=p_codes[b][:, P * block : P * (block + count)].bitcast(I32),
             )
 
-        def store_scales(b0, b1):
-            for q in range(4):
+        def store_scales(first_image, end_image):
+            m = slice(first_image * N, end_image * N)
+            for quadrant in range(4):
                 nc.sync.dma_start(
-                    out=out_2[0, 4 * q : 4 * q + 4, N * b0 : N * b1].bitcast(I32),
-                    in_=p_scales[32 * q : 32 * q + 4, N * b0 : N * b1].bitcast(I32),
+                    out=out_2[0, 4 * quadrant : 4 * quadrant + 4, m].bitcast(I32),
+                    in_=out_plane[32 * quadrant : 32 * quadrant + 4, m].bitcast(I32),
                 )
 
-        vcopy, scopy = nc.vector.tensor_copy, nc.scalar.copy
-        for j in range(4):
-            scale_rows(0, j)
-        cg4f = const.tile([P, PACK], F32, name="cg4f")
-        nc.vector.tensor_copy(out=rows_f[:], in_=rows[:])
-        c_ps = psum.tile([P, P], F32, name="c_ps", tag="m_ps", bufs=2)
-        nc.tensor.transpose(c_ps[:], rows_f[:], ident[:])
-        nc.vector.tensor_copy(out=cols[:, 0:8], in_=c_ps[:, 0:8])
-        nc.vector.tensor_tensor(out=cols[:, 8:16], in0=cols[:, 0:8], in1=cols[:, 0:8], op=MUL)
-        nc.vector.tensor_copy(out=cg4f[:], in_=cg4[:])
-        sr2_ps = psum.tile([P, N], F32, name="sr2_ps", tag="x_ps", bufs=2)
-        sr_ps = psum.tile([P, N], F32, name="sr_ps", tag="x_ps", bufs=2)
-        for t in range(4):
-            nc.tensor.transpose(
-                sr2_ps[:, P * t : P * t + P], cols[:, 12 + t : 13 + t].to_broadcast([P, P]), ident[:]
-            )
-        for t in range(4):
-            nc.tensor.transpose(sr_ps[:, P * t : P * t + P], cols[:, 4 + t : 5 + t].to_broadcast([P, P]), ident[:])
-        inv = const.tile([P, 4, N], F32, name="inv")
+        filter_psum = {}
 
-        def invert(t):
+        def spread_vectors():
+            nc.vector.tensor_copy(out=vectors_f32[:], in_=vectors[:])
+            columns_psum = psum.tile([P, P], F32, name="columns_psum", tag="turned", bufs=2)
+            nc.tensor.transpose(columns_psum[:], vectors_f32[:], identity[:])
+            nc.vector.tensor_copy(out=columns[:, 0:8], in_=columns_psum[:, 0:8])
+            nc.vector.tensor_tensor(out=columns[:, 8:16], in0=columns[:, 0:8], in1=columns[:, 0:8], op=MULT)
+            filter_psum["sr squared"] = psum.tile([P, N], F32, name="sr2_psum", tag="m_psum", bufs=3)
+            filter_psum["sr"] = psum.tile([P, N], F32, name="sr_psum", tag="turned", bufs=2)
+            for name, first in (("sr squared", 12), ("sr", 4)):
+                for i in range(BLOCKS):
+                    column = columns[:, first + i : first + i + 1]
+                    nc.tensor.transpose(
+                        filter_psum[name][:, P * i : P * i + P], column.to_broadcast([P, P]), identity[:]
+                    )
+
+        def invert(block):
             nc.scalar.activation(
-                out=inv[:, t, :],
-                in_=sr2_ps[:],
+                out=inverse[:, block, :],
+                in_=filter_psum["sr squared"][:],
                 func=ACT.Abs_reciprocal_sqrt,
                 bias=TIKHONOV,
-                scale=cols[:, 8 + t : 9 + t],
+                scale=columns[:, 8 + block : 9 + block],
+            )
+            nc.scalar.activation(out=inverse[:, block, :], in_=inverse[:, block, :], func=ACT.Square)
+
+        def make_gain(block):
+            nc.vector.tensor_tensor(
+                out=gain[:, block, :], in0=filter_psum["sr"][:], in1=inverse[:, block, :], op=MULT
             )
 
-        def square(t):
-            nc.scalar.activation(out=inv[:, t, :], in_=inv[:, t, :], func=ACT.Square)
-
-        def make_filter(t):
-            nc.vector.tensor_tensor(out=filt[:, t, :], in0=sr_ps[:], in1=inv[:, t, :], op=MUL)
-
-        for h in range(4):
-            interleave(0, h, vcopy)
+        scale_rows(0)
+        spread_vectors()
         invert(0)
-        square(0)
-        make_filter(0)
-        quant_a(0)
-        for j in range(4):
-            scale_rows(1, j)
-        for h in range(2):
-            interleave(1, h, vcopy)
-        interleave(1, 2, scopy)
+        group_rows(0, 0, nc.vector.tensor_copy)
+        group_rows(0, 1, nc.vector.tensor_copy)
+        scale_rows(1)
+        quantize_a(0)
+        make_gain(0)
+        nc.vector.tensor_copy(out=cg_f32[:], in_=cg_words[:])
+        for block in BLOCK_ORDER[:3]:
+            first_matmul(0, block)
         invert(1)
-        square(1)
-        interleave(1, 3, scopy)
-        invert(2)
-        square(2)
-        invert(3)
-        square(3)
+        group_rows(1, 0, nc.vector.tensor_copy)
+        group_rows(1, 1, nc.scalar.copy)
+        for block in (2, 3):
+            invert(block)
+        scale_rows(2)
 
-        PAIRS = CHUNKS // 2
-        for i in range(-3, PAIRS + 2):
-            if 0 <= i - 1 < PAIRS:
-                turn(i - 1)
-            for c in range(2):
-                if 0 <= i < PAIRS:
-                    filter_out(2 * i + c)
-                    round_out(2 * i + c)
-            if 0 <= i < PAIRS:
-                store_out(i)
-            if 0 <= i + 2 < PAIRS:
-                make_d(2 * i + 4)
-                make_d(2 * i + 5)
-            if 0 <= i + 1 < PAIRS:
-                quant_d(i + 1)
-                mx2(2 * i + 2)
-                mx2(2 * i + 3)
-            if i in (-1, 0):
-                for t in (1,) if i < 0 else (2, 3):
-                    make_filter(t)
-            if 0 <= i - 2 < PAIRS:
-                quant_out(i - 2)
-                b, h = divmod(i - 2, 2)
-                if h == 1:
-                    store_codes(b)
-                    if b in (3, 5, 6, 7):
-                        store_scales({3: 0, 5: 4, 6: 6, 7: 7}[b], b + 1)
-            if i % 2 == 1 and 1 <= (i + 3) // 2 < B:
-                quant_a((i + 3) // 2)
-            if 0 <= i + 3 < PAIRS:
-                mx1(2 * i + 6)
-                mx1(2 * i + 7)
-            if 0 <= i - 1 < PAIRS:
-                gather_out(i - 1)
-            nb, h = divmod(i + 5, 2)
-            if 1 <= nb < B:
-                for hh in (2 * h, 2 * h + 1):
-                    if nb > 1:
-                        interleave(nb, hh, scopy)
-            nb, h = divmod(i + 7, 2)
-            if 2 <= nb < B:
-                scale_rows(nb, 2 * h)
-                scale_rows(nb, 2 * h + 1)
+        for b in range(-1, B - 1):
+            started = b >= 0
+            if started:
+                filter_block(b, 0)
+                second_matmul(b, 3)
+                filter_block(b, 1)
+                store_result(b, 0, 2)
+                filter_block(b, 2)
+                filter_block(b, 3)
+                store_result(b, 2, 2)
+            make_d(b + 1, BLOCK_ORDER[0])
+            first_matmul(b + 1, BLOCK_ORDER[3])
+            if started:
+                round_gpsimd(b, 1)
+                round_scalar(b, 0)
+                turn(b, 0, 2)
+            if b + 3 < B:
+                group_rows(b + 3, 0, nc.scalar.copy)
+            for block in BLOCK_ORDER[1:]:
+                make_d(b + 1, block)
+            if b + 2 < B:
+                quantize_a(b + 2)
+            quantize_d(b + 1)
+            if not started:
+                for block in (1, 2, 3):
+                    make_gain(block)
+            if started:
+                round_gpsimd(b, 2)
+                round_gpsimd(b, 3)
+            if b + 4 < B:
+                scale_rows(b + 4)
+            if b + 3 < B:
+                group_rows(b + 3, 1, nc.scalar.copy)
+            if started:
+                turn(b, 2, 2)
+                group_out(b, 0, 2)
+            if b >= 1:
+                quantize_out(b - 1, 0, BLOCKS)
+                store_codes(b - 1, 0, BLOCKS)
+                if b == 4:
+                    store_scales(0, b)
+                if b == 6:
+                    store_scales(4, b)
+            if b + 2 < B:
+                first_matmul(b + 2, BLOCK_ORDER[0])
+            second_matmul(b + 1, 0)
+            second_matmul(b + 1, 1)
+            if started:
+                group_out(b, 2, 2)
+            second_matmul(b + 1, 2)
+            if b + 2 < B:
+                first_matmul(b + 2, BLOCK_ORDER[1])
+                first_matmul(b + 2, BLOCK_ORDER[2])
+
+        b = B - 1
+        for block in range(BLOCKS):
+            filter_block(b, block)
+            if block == 0:
+                second_matmul(b, 3)
+                round_scalar(b, block)
+            elif block == BLOCKS - 1:
+                nc.vector.tensor_copy(out=rounded[b][:, block, :], in_=result[b][:, block, :])
+            else:
+                round_gpsimd(b, block)
+            if block == 1:
+                quantize_out(b - 1, 0, BLOCKS)
+                store_codes(b - 1, 0, BLOCKS)
+                store_result(b, 0, 2)
+            if block == BLOCKS - 1:
+                store_result(b, 2, 1)
+                store_result(b, 3, 1)
+            turn(b, block, 1)
+            group_out(b, block, 1)
+        for block in (0, 2):
+            quantize_out(b, block, 2)
+            store_codes(b, block, 2)
+        store_scales(6, B)

from contextlib import ExitStack

import concourse.mybir as mybir
from concourse.masks import make_identity

B = 8
N = 512
P = 128
WORD = 4
BLOCKS = N // P
TIKHONOV = 0.3
FLOPS = 2 * 2 * B * N * N * N

F32 = mybir.dt.float32
BF16 = mybir.dt.bfloat16
I32 = mybir.dt.int32
U32 = mybir.dt.uint32
U8 = mybir.dt.uint8
FP8X4 = mybir.dt.float8_e4m3fn_x4
ACT = mybir.ActivationFunctionType
MULT = mybir.AluOpType.mult

BLOCK_ORDER = (3, 0, 1, 2)


def scalar_blocks(b):
    if b == 0:
        return ()
    if b >= B - 2:
        return (3, 2)
    return (3,)


def tile_separablelenslesstikhonovcoefficients_x2_kernel(
    tc, y, rg, ul_words, ul_scales, cg, ur_words, ur_scales, sl, sr, out_0, out_1, out_2
):
    nc = tc.nc
    with ExitStack() as ctx:
        const = ctx.enter_context(tc.tile_pool(name="const", bufs=1))
        loads = ctx.enter_context(tc.tile_pool(name="loads", bufs=B))
        work = ctx.enter_context(tc.tile_pool(name="work", bufs=2))
        psum = ctx.enter_context(tc.psum_pool(name="psum", bufs=2))
        ctx.enter_context(tc.manual_schedule())

        identity = const.tile([P, P], F32, name="identity")
        vectors = const.tile([P, P], BF16, name="vectors")
        vectors_f32 = const.tile([P, P], F32, name="vectors_f32")
        columns = const.tile([P, 16], F32, name="columns")
        rg_words = const.tile([P, WORD], BF16, name="rg_words")
        cg_words = const.tile([P, WORD], BF16, name="cg_words")
        cg_f32 = const.tile([P, WORD], F32, name="cg_f32")
        ul_codes = const.tile([P, N], U32, name="ul_codes", align_bytes=64)
        ul_plane = const.tile([P, N], U8, name="ul_plane", align_bytes=64)
        ur_codes = const.tile([P, N], U32, name="ur_codes", align_bytes=64)
        ur_plane = const.tile([P, N], U8, name="ur_plane", align_bytes=64)
        inverse = const.tile([P, BLOCKS, N], F32, name="inverse")
        gain = const.tile([P, BLOCKS, N], F32, name="gain")
        out_plane = const.tile([P, B * N], U8, name="out_plane", align_bytes=64)

        nc.vector.memset(vectors[:], 0.0)
        nc.vector.memset(ul_plane[:].bitcast(I32), 0)
        nc.vector.memset(ur_plane[:].bitcast(I32), 0)
        make_identity(nc, identity[:])

        y_rows = {}

        def load_image(b, pieces):
            y_tile = loads.tile([P, WORD, N], BF16, name="y_tile")
            y_rows[b] = y_tile
            rows = y[b].rearrange("(i j) q -> i j q", j=WORD)
            step = WORD // pieces
            for j in range(0, WORD, step):
                nc.sync.dma_start(out=y_tile[:, j : j + step, :], in_=rows[:, j : j + step, :])

        def load_words(codes, dram):
            nc.sync.dma_start(out=codes[:].bitcast(I32), in_=dram[0].rearrange("i n t -> i (n t)").bitcast(I32))

        def load_scales(queue, plane, dram):
            for quadrant in range(4):
                queue.dma_start(
                    out=plane[32 * quadrant : 32 * quadrant + 4, :].bitcast(I32),
                    in_=dram[0, 4 * quadrant : 4 * quadrant + 4, :].bitcast(I32),
                )

        nc.scalar.dma_start(out=rg_words[:], in_=rg.rearrange("(i j) -> i j", j=WORD))
        nc.scalar.dma_start(out=vectors[0:4, :], in_=sl.rearrange("(r c) -> r c", c=P))
        nc.scalar.dma_start(out=vectors[4:8, :], in_=sr.rearrange("(r c) -> r c", c=P))
        load_image(0, WORD)
        load_words(ul_codes, ul_words)
        nc.gpsimd.dma_start(out=cg_words[:], in_=cg.rearrange("(i j) -> i j", j=WORD))
        load_scales(nc.sync, ul_plane, ul_scales)
        load_image(1, 1)
        load_words(ur_codes, ur_words)
        load_scales(nc.gpsimd, ur_plane, ur_scales)
        for b in range(2, B):
            load_image(b, 1)

        a_scaled, a_grouped, a_codes, a_plane = {}, {}, {}, {}

        def scale_rows(b):
            a_scaled[b] = work.tile([P, WORD, N], BF16, name="a_scaled", bufs=3)
            for j in range(WORD):
                nc.vector.tensor_scalar(
                    out=a_scaled[b][:, j, :],
                    in0=y_rows[b][:, j, :],
                    scalar1=rg_words[:, j : j + 1],
                    scalar2=None,
                    op0=MULT,
                )

        def group_rows(b, half, copy):
            if half == 0:
                a_grouped[b] = work.tile([P, WORD * N], BF16, name="a_grouped", align_bytes=64, bufs=3)
            i = slice(64 * half, 64 * half + 64)
            copy(
                out=a_grouped[b][:].rearrange("p (t i j) -> p i j t", t=WORD, j=WORD)[:, i, :, :],
                in_=a_scaled[b][:].rearrange("p j (i t) -> p i j t", t=WORD)[:, i, :, :],
            )

        def quantize_a(b):
            a_codes[b] = work.tile([P, N], U32, name="a_codes", align_bytes=64)
            a_plane[b] = work.tile([P, N], U8, name="a_plane", align_bytes=64)
            nc.vector.quantize_mx(out=a_codes[b][:].bitcast(FP8X4), scales=a_plane[b][:], in_=a_grouped[b][:])

        t_psum, d_grouped, d_codes, d_plane = {}, {}, {}, {}

        def first_matmul(b, block):
            t_psum[b, block] = psum.tile([P, WORD, P], F32, name="t_psum", bufs=3)
            k = slice(P * block, P * block + P)
            for t in range(WORD):
                columns_q = slice(P * t, P * t + P)
                nc.tensor.matmul_mx(
                    out=t_psum[b, block][:, t, :],
                    lhsT=a_codes[b][:, columns_q].bitcast(FP8X4),
                    lhsT_scale=a_plane[b][:, columns_q],
                    rhs=ul_codes[:, k].bitcast(FP8X4),
                    rhs_scale=ul_plane[:, k],
                    start=True,
                    stop=True,
                )

        def d_block(b, block):
            if b not in d_grouped:
                d_grouped[b] = work.tile([P, N, WORD], BF16, name="d_grouped", align_bytes=64)
            return d_grouped[b][:, P * block : P * block + P, :]

        def make_d_vector(b, block):
            nc.vector.tensor_tensor(
                out=d_block(b, block),
                in0=t_psum[b, block][:].rearrange("p t k -> p k t"),
                in1=cg_words[:].unsqueeze(1).to_broadcast([P, P, WORD]),
                op=MULT,
            )

        def make_d_scalar(b, block):
            d_rows = work.tile([P, WORD, P], BF16, name="d_rows")
            for t in range(WORD):
                nc.scalar.activation(
                    out=d_rows[:, t, :], in_=t_psum[b, block][:, t, :], func=ACT.Copy, scale=cg_f32[:, t : t + 1]
                )
            nc.scalar.copy(out=d_block(b, block), in_=d_rows[:].rearrange("p t k -> p k t"))

        def make_d(b, block):
            if block in scalar_blocks(b):
                make_d_scalar(b, block)
            else:
                make_d_vector(b, block)

        def quantize_d(b):
            d_codes[b] = work.tile([P, N], U32, name="d_codes", align_bytes=64)
            d_plane[b] = work.tile([P, N], U8, name="d_plane", align_bytes=64)
            nc.vector.quantize_mx(
                out=d_codes[b][:].bitcast(FP8X4),
                scales=d_plane[b][:],
                in_=d_grouped[b][:].rearrange("p k t -> p (k t)"),
            )

        m_psum, result, rounded = {}, {}, {}

        def second_matmul(b, block):
            k = slice(P * block, P * block + P)
            m_psum[b, block] = psum.tile([P, N], F32, name="m_psum", bufs=3)
            nc.tensor.matmul_mx(
                out=m_psum[b, block][:],
                lhsT=d_codes[b][:, k].bitcast(FP8X4),
                lhsT_scale=d_plane[b][:, k],
                rhs=ur_codes[:].bitcast(FP8X4),
                rhs_scale=ur_plane[:],
                start=True,
                stop=True,
            )

        def filter_block(b, block):
            if block == 0:
                result[b] = work.tile([P, BLOCKS, N], F32, name="result", bufs=3)
                rounded[b] = work.tile([P, BLOCKS, N], BF16, name="rounded")
            nc.vector.scalar_tensor_tensor(
                out=result[b][:, block, :],
                in0=m_psum[b, block][:],
                scalar=columns[:, block : block + 1],
                in1=gain[:, block, :],
                op0=MULT,
                op1=MULT,
            )

        def store_result(b, block, count):
            nc.sync.dma_start(
                out=out_0[b, P * block : P * (block + count), :].rearrange("(c k) l -> k c l", c=count),
                in_=result[b][:, block : block + count, :],
            )

        turned, p_grouped, p_codes = {}, {}, {}

        def round_scalar(b, block):
            nc.scalar.copy(out=rounded[b][:, block, :], in_=result[b][:, block, :])

        def round_gpsimd(b, block):
            nc.gpsimd.tensor_scalar(
                out=rounded[b][:, block, :],
                in0=result[b][:, block, :],
                scalar1=1.0,
                scalar2=1.0,
                op0=MULT,
                op1=MULT,
            )

        def turn(b, block, count):
            turned[b, block] = psum.tile([P, count, 2, P], F32, name="turned", bufs=2)
            for c in range(count):
                words = rounded[b][:, block + c, :].bitcast(F32)
                for u in range(2):
                    nc.tensor.transpose(turned[b, block][:, c, u, :], words[:, u::2], identity[:])

        def group_out(b, block, count):
            if block == 0:
                p_grouped[b] = work.tile([P, N * WORD], BF16, name="p_grouped", align_bytes=64)
            values = slice(P * WORD * block, P * WORD * (block + count))
            nc.scalar.copy(
                out=p_grouped[b][:, values].bitcast(F32).rearrange("p (c k u) -> p c k u", c=count, u=2),
                in_=turned[b, block][:].rearrange("p c u k -> p c k u"),
            )

        def quantize_out(b, block, count):
            if block == 0:
                p_codes[b] = work.tile([P, N], U32, name="p_codes", align_bytes=64)
            k = slice(P * block, P * (block + count))
            nc.vector.quantize_mx(
                out=p_codes[b][:, k].bitcast(FP8X4),
                scales=out_plane[:, b * N + P * block : b * N + P * (block + count)],
                in_=p_grouped[b][:, P * WORD * block : P * WORD * (block + count)],
            )

        def store_codes(b, block, count):
            first, last = b * N + P * block, b * N + P * (block + count)
            nc.sync.dma_start(
                out=out_1[0].rearrange("i m t -> i (m t)")[:, WORD * first : WORD * last].bitcast(I32),
                in_=p_codes[b][:, P * block : P * (block + count)].bitcast(I32),
            )

        def store_scales(first_image, end_image):
            m = slice(first_image * N, end_image * N)
            for quadrant in range(4):
                nc.sync.dma_start(
                    out=out_2[0, 4 * quadrant : 4 * quadrant + 4, m].bitcast(I32),
                    in_=out_plane[32 * quadrant : 32 * quadrant + 4, m].bitcast(I32),
                )

        filter_psum = {}

        def spread_vectors():
            nc.vector.tensor_copy(out=vectors_f32[:], in_=vectors[:])
            columns_psum = psum.tile([P, P], F32, name="columns_psum", tag="turned", bufs=2)
            nc.tensor.transpose(columns_psum[:], vectors_f32[:], identity[:])
            nc.vector.tensor_copy(out=columns[:, 0:8], in_=columns_psum[:, 0:8])
            nc.vector.tensor_tensor(out=columns[:, 8:16], in0=columns[:, 0:8], in1=columns[:, 0:8], op=MULT)
            filter_psum["sr squared"] = psum.tile([P, N], F32, name="sr2_psum", tag="m_psum", bufs=3)
            filter_psum["sr"] = psum.tile([P, N], F32, name="sr_psum", tag="turned", bufs=2)
            for name, first in (("sr squared", 12), ("sr", 4)):
                for i in range(BLOCKS):
                    column = columns[:, first + i : first + i + 1]
                    nc.tensor.transpose(
                        filter_psum[name][:, P * i : P * i + P], column.to_broadcast([P, P]), identity[:]
                    )

        def invert(block):
            nc.scalar.activation(
                out=inverse[:, block, :],
                in_=filter_psum["sr squared"][:],
                func=ACT.Abs_reciprocal_sqrt,
                bias=TIKHONOV,
                scale=columns[:, 8 + block : 9 + block],
            )
            nc.scalar.activation(out=inverse[:, block, :], in_=inverse[:, block, :], func=ACT.Square)

        def make_gain(block):
            nc.vector.tensor_tensor(
                out=gain[:, block, :], in0=filter_psum["sr"][:], in1=inverse[:, block, :], op=MULT
            )

        scale_rows(0)
        spread_vectors()
        invert(0)
        group_rows(0, 0, nc.vector.tensor_copy)
        group_rows(0, 1, nc.vector.tensor_copy)
        scale_rows(1)
        quantize_a(0)
        make_gain(0)
        nc.vector.tensor_copy(out=cg_f32[:], in_=cg_words[:])
        for block in BLOCK_ORDER[:3]:
            first_matmul(0, block)
        invert(1)
        group_rows(1, 0, nc.vector.tensor_copy)
        group_rows(1, 1, nc.scalar.copy)
        for block in (2, 3):
            invert(block)
        scale_rows(2)

        for b in range(-1, B - 1):
            started = b >= 0
            if started:
                filter_block(b, 0)
                second_matmul(b, 3)
                filter_block(b, 1)
                store_result(b, 0, 2)
                filter_block(b, 2)
                filter_block(b, 3)
                store_result(b, 2, 2)
            make_d(b + 1, BLOCK_ORDER[0])
            first_matmul(b + 1, BLOCK_ORDER[3])
            if started:
                round_gpsimd(b, 1)
                round_scalar(b, 0)
                turn(b, 0, 2)
            if b + 3 < B:
                group_rows(b + 3, 0, nc.scalar.copy)
            for block in BLOCK_ORDER[1:]:
                make_d(b + 1, block)
            if b + 2 < B:
                quantize_a(b + 2)
            quantize_d(b + 1)
            if not started:
                for block in (1, 2, 3):
                    make_gain(block)
            if started:
                round_gpsimd(b, 2)
                round_gpsimd(b, 3)
            if b + 4 < B:
                scale_rows(b + 4)
            if b + 3 < B:
                group_rows(b + 3, 1, nc.scalar.copy)
            if started:
                turn(b, 2, 2)
                group_out(b, 0, 2)
            if b >= 1:
                quantize_out(b - 1, 0, BLOCKS)
                store_codes(b - 1, 0, BLOCKS)
                if b == 4:
                    store_scales(0, b)
                if b == 6:
                    store_scales(4, b)
            if b + 2 < B:
                first_matmul(b + 2, BLOCK_ORDER[0])
            second_matmul(b + 1, 0)
            second_matmul(b + 1, 1)
            if started:
                group_out(b, 2, 2)
            second_matmul(b + 1, 2)
            if b + 2 < B:
                first_matmul(b + 2, BLOCK_ORDER[1])
                first_matmul(b + 2, BLOCK_ORDER[2])

        b = B - 1
        for block in range(BLOCKS):
            filter_block(b, block)
            if block == 0:
                second_matmul(b, 3)
                round_scalar(b, block)
            elif block == BLOCKS - 1:
                nc.vector.tensor_copy(out=rounded[b][:, block, :], in_=result[b][:, block, :])
            else:
                round_gpsimd(b, block)
            if block == 1:
                quantize_out(b - 1, 0, BLOCKS)
                store_codes(b - 1, 0, BLOCKS)
                store_result(b, 0, 2)
            if block == BLOCKS - 1:
                store_result(b, 2, 1)
                store_result(b, 3, 1)
            turn(b, block, 1)
            group_out(b, block, 1)
        for block in (0, 2):
            quantize_out(b, block, 2)
            store_codes(b, block, 2)
        store_scales(6, B)
